import numpy as np
import ml_dtypes


def mxq(x, axis, fmt="e4m3"):
    dtype, down = {"e4m3": (ml_dtypes.float8_e4m3fn, 7), "e5m2": (ml_dtypes.float8_e5m2, 14)}[fmt]
    v = np.moveaxis(np.asarray(x, np.float32).astype(ml_dtypes.bfloat16).astype(np.float64), axis, -1)
    blocks = v.reshape(v.shape[:-1] + (-1, 32))
    amax = np.abs(blocks).max(-1, keepdims=True)
    byte = np.maximum(np.where(amax > 0, np.frexp(amax)[1] - 1 + 127, 0) - down, 1)
    scale = np.exp2(byte - 127.0)
    codes = (blocks / scale).astype(np.float32).astype(dtype).astype(np.float64)
    return np.moveaxis((codes * scale).reshape(v.shape), -1, axis)


WIDE = False


def mx_kscale(k):
    if not WIDE:
        return np.ones(k)
    levels = np.array([10, -10, 5, -5, 0])
    if k % 512:
        return np.exp2(np.random.permutation(np.resize(levels, k // 32))).repeat(32)
    a = np.empty((k // 512, 16))
    for p in range(k // 512):
        a[p, :8] = np.random.permutation(np.resize(levels, 8))
        for g in range(8):
            far = levels[np.abs(levels - a[p, g]) >= 10]
            a[p, g + 8] = far[np.random.randint(len(far))]
    return np.exp2(a.ravel()).repeat(32)


def f64(x):
    return np.asarray(x).astype(np.float64)


def striped(idx):
    return np.tile(idx.reshape(-1, 16).T, (8, 1)).astype(np.uint16)


def unstriped(offs):
    return offs[:16].T.reshape(-1).astype(np.int64)


def striped8(idx):
    return np.concatenate([x.reshape(-1, 16).T for x in idx]).astype(np.uint16)


def runs(offs, k):
    lists = np.stack([offs[16 * r : 16 * r + 16].T.reshape(-1) for r in range(8)]).astype(np.int64)
    return lists[np.arange(k) % 512 // 64]


def pack_weight(w):
    k, n = w.shape
    w = f64(np.asarray(w, np.float32).astype(ml_dtypes.bfloat16)).reshape(k // 32, 32, n)
    amax = np.abs(w).max(1)
    byte = np.clip(np.where(amax > 0, np.frexp(amax)[1] - 1 + 127 - 7, 1), 1, 254)
    scaled = (w * np.exp2(127.0 - byte)[:, None, :]).reshape(k, n).astype(np.float32)
    words = np.ascontiguousarray(scaled.reshape(k // 512, 128, 4, n).transpose(0, 1, 3, 2)).astype(ml_dtypes.float8_e4m3fn).view(np.uint8)
    return words, np.ascontiguousarray(byte.astype(np.uint8).reshape(k // 512, 16, n))


def unpack_weight(words, scales):
    g, p, n, _ = words.shape
    vals = np.ascontiguousarray(words).view(ml_dtypes.float8_e4m3fn).astype(np.float64) * np.repeat(np.exp2(scales.astype(np.float64) - 127.0), 8, axis=1)[..., None]
    return vals.transpose(0, 1, 3, 2).reshape(g * 512, n)


E2M1 = np.array([0.0, 0.5, 1.0, 1.5, 2.0, 3.0, 4.0, 6.0, -0.0, -0.5, -1.0, -1.5, -2.0, -3.0, -4.0, -6.0])


def pack_fp4(w):
    k, n = w.shape
    w = f64(np.asarray(w, np.float32).astype(ml_dtypes.bfloat16)).reshape(k // 32, 32, n)
    amax = np.abs(w).max(1)
    mant, ex = np.frexp(amax / 6.0)
    byte = np.clip(np.where(amax > 0, np.where(mant > 0.5, ex, ex - 1) + 127, 1), 1, 254)
    scaled = (w * np.exp2(127.0 - byte)[:, None, :]).reshape(k, n).astype(np.float32)
    c = np.ascontiguousarray(scaled.reshape(k // 512, 128, 4, n).transpose(0, 1, 3, 2)).astype(ml_dtypes.float4_e2m1fn).view(np.uint8) & 0xF
    words = (c[..., 0::2] | (c[..., 1::2] << 4)).reshape(k // 512, 128, 2 * n)
    return np.ascontiguousarray(words), np.ascontiguousarray(byte.astype(np.uint8).reshape(k // 512, 16, n))


def unpack_fp4(words, scales):
    g, _, n = scales.shape
    words = np.ascontiguousarray(words).reshape(g, 128, n, 2)
    nib = np.empty((g, 128, n, 4), np.uint8)
    nib[..., 0::2] = words & 0xF
    nib[..., 1::2] = words >> 4
    vals = E2M1[nib] * np.repeat(np.exp2(scales.astype(np.float64) - 127.0), 8, axis=1)[..., None]
    return vals.transpose(0, 1, 3, 2).reshape(g * 512, n)


def sigmoid(v):
    return 1.0 / (1.0 + np.exp(-np.maximum(v, -700.0)))

def planes(y):
    n, m = y.shape
    v = y.astype(np.float32).astype(ml_dtypes.bfloat16).astype(np.float64).reshape(n // 32, 32, m)
    top = np.abs(v).max(1)
    byte = np.clip(np.where(top > 0, np.frexp(top)[1] - 1 + 127 - 7, 1), 1, 254)
    codes = (v * np.exp2(127.0 - byte)[:, None, :]).reshape(n, m).astype(np.float32).astype(ml_dtypes.float8_e4m3fn).view(np.uint8)
    words = codes.reshape(n // 512, 128, 4, m).transpose(0, 1, 3, 2)
    return np.ascontiguousarray(words), np.ascontiguousarray(byte.astype(np.uint8).reshape(n // 512, 16, m))


K, T, S, N, G, H, W = 512, 2048, 512, 512, 2048, 512, 384


def setup_inputs():
    n = np.random.standard_normal
    s = mx_kscale(K)[:, None]
    u = mx_kscale(S)
    packed_xT = pack_weight(n((K, T)) * s)
    packed_dT = pack_weight(n((K, G)) / s)
    packed_w1 = pack_fp4(n((H, N)) / np.sqrt(H) / u[:, None])
    return {
        "x_words": packed_xT[0],
        "x_scales": packed_xT[1],
        "d_words": packed_dT[0],
        "d_scales": packed_dT[1],
        "gn": (np.random.uniform(0.5, 1.5, (H, 1)) * u[:, None]).astype(np.float32),
        "w1_words": packed_w1[0],
        "w1_scales": packed_w1[1],
        "offs": striped(np.random.permutation(T)[:S]),
        "k1": striped8(np.random.randint(0, G, (8, H))),
        "n1": striped(np.random.permutation(S)[:W]),
        "n2": striped(np.random.permutation(S)[:W]),
        "n3": striped8(np.stack([np.random.permutation(S) for _ in range(8)])),
    }


def reference(x_words, x_scales, d_words, d_scales, gn, w1_words, w1_scales, offs, k1, n1, n2, n3):
    d_k1 = unpack_weight(d_words, d_scales)[np.arange(K)[:, None], runs(k1, K)]
    xq = unpack_weight(x_words, x_scales)[:, unstriped(offs)]
    h = 0.0625 * (d_k1.T @ xq)
    pa = h[:, unstriped(n2)]
    old = h[:, unstriped(n1)]
    ra = np.minimum(pa, old) - (0.5 * pa)
    ds = h.copy()
    ds[:, unstriped(n1)] = ra
    z = f64(gn) * ds
    h2 = unpack_fp4(w1_words, w1_scales).T @ mxq(z, 0, "e4m3")
    out_0 = h2 * (sigmoid(h2[np.arange(N)[:, None], runs(n3, N)]))
    return (out_0,) + planes(out_0)

@@ -1,0 +1,203 @@
+from contextlib import ExitStack
+
+import concourse.mybir as mybir
+
+K, T, S, N, G, H, W = 512, 2048, 512, 512, 2048, 512, 384
+FLOPS = 2 * K * H * S + 2 * H * N * S
+
+F32 = mybir.dt.float32
+BF16 = mybir.dt.bfloat16
+I32 = mybir.dt.int32
+U32 = mybir.dt.uint32
+U16 = mybir.dt.uint16
+U8 = mybir.dt.uint8
+FP8X4 = mybir.dt.float8_e4m3fn_x4
+FP4X4 = mybir.dt.float4_e2m1fn_x4
+ALU = mybir.AluOpType
+ACT = mybir.ActivationFunctionType
+
+P = 128
+PACK = 4
+HALF = S // 2
+
+
+def tile_picked_pqlaykmingate_none_po_kernel(
+    tc, x_words, x_scales, d_words, d_scales, gn, w1_words, w1_scales, offs, k1, n1, n2, n3, out_0, out_1, out_2
+):
+    nc = tc.nc
+    with ExitStack() as ctx:
+        keep = ctx.enter_context(tc.tile_pool(name="keep", bufs=1))
+        psum = ctx.enter_context(tc.psum_pool(name="psum", bufs=1))
+
+        def sb(name, shape, dtype, tag=None):
+            return keep.tile(shape, dtype, name=name, tag=tag or name, align_bytes=64)
+
+        k1_t = sb("k1_t", [P, H // 16], U16)
+        offs_t = sb("offs_t", [P, S // 16], U16)
+        n1_t = sb("n1_t", [P, W // 16], U16)
+        n2_t = sb("n2_t", [P, W // 16], U16)
+        n3_t = sb("n3_t", [P, S // 16], U16)
+        d_w = sb("d_w", [P, G], U32)
+        x_w = sb("x_w", [P, T], U32)
+        d_s = sb("d_s", [P, G], U8)
+        x_s = sb("x_s", [P, T], U8)
+        w_w = sb("w_w", [P, 2 * N], U8)
+        gain = sb("gain", [P, PACK], F32)
+
+        nc.vector.memset(d_s[:].bitcast(I32), 0)
+        nc.vector.memset(x_s[:].bitcast(I32), 0)
+
+        nc.sync.dma_start(k1_t[:], k1)
+        nc.sync.dma_start(d_w[:].bitcast(I32), d_words[0].rearrange("p n t -> p (n t)").bitcast(I32))
+        for r in range(2):
+            nc.scalar.dma_start(d_s[r:P:16, :].bitcast(I32), d_scales[0][r:16:2, :].bitcast(I32))
+        nc.sync.dma_start(offs_t[:], offs)
+        nc.sync.dma_start(n2_t[:], n2)
+        nc.sync.dma_start(n1_t[:], n1)
+        nc.sync.dma_start(n3_t[:], n3)
+        nc.sync.dma_start(x_w[:].bitcast(I32), x_words[0].rearrange("p n t -> p (n t)").bitcast(I32))
+        for r in range(4):
+            nc.scalar.dma_start(x_s[r:P:32, :].bitcast(I32), x_scales[0][r:16:4, :].bitcast(I32))
+        nc.gpsimd.dma_start(w_w[:].bitcast(I32), w1_words[0].bitcast(I32))
+        nc.gpsimd.dma_start(gain[:], gn.rearrange("(p t) o -> p (t o)", t=PACK))
+
+        d_sg = sb("d_sg", [P, H], U8, tag="picked")
+        d_sd = sb("d_sd", [P, H], U8)
+        d_sp = sb("d_sp", [P, H], U8)
+        nc.vector.tensor_copy(d_sg[:], d_s[:].indirect(k1_t[:]))
+        nc.vector.tensor_copy(d_sd[:].rearrange("p (t m) -> p t m", t=PACK), d_sg[:].rearrange("p (m t) -> p t m", t=PACK))
+        nc.vector.tensor_copy(d_sp[:].bitcast(I32), d_sd[:].bitcast(I32))
+        for r in range(2):
+            nc.scalar.dma_start(d_sp[2 + r : P : 32, :].bitcast(I32), d_sd[16 + r : P : 32, :].bitcast(I32))
+
+        w_s = sb("w_s", [P, N], U8, tag="d_sd")
+        nc.gpsimd.memset(w_s[:].bitcast(I32), 0)
+        for r in range(4):
+            nc.sync.dma_start(w_s[r:P:32, :].bitcast(I32), w1_scales[0][r:16:4, :].bitcast(I32))
+
+        d_wg = sb("d_wg", [P, H], U32, tag="picked")
+        d_wd = sb("d_wd", [P, H], U32)
+        nc.vector.tensor_copy(d_wg[:], d_w[:].indirect(k1_t[:]))
+        nc.vector.tensor_copy(
+            d_wd[:].bitcast(I32).rearrange("p (t m) -> p t m", t=PACK),
+            d_wg[:].bitcast(I32).rearrange("p (m t) -> p t m", t=PACK),
+        )
+        x_sg = sb("x_sg", [P, S], U8, tag="picked")
+        nc.vector.tensor_copy(x_sg[:], x_s[:].indirect(offs_t[:]))
+        x_wg = sb("x_wg", [P, S], U32, tag="x_s")
+        for u in range(2):
+            nc.vector.tensor_copy(
+                x_wg[:, u * HALF : (u + 1) * HALF], x_w[:].indirect(offs_t[:, u * HALF // 16 : (u + 1) * HALF // 16])
+            )
+
+        banks = [psum.tile([P, S], F32, name=f"bank{t}") for t in range(PACK)]
+        for t in range(PACK):
+            cols = slice(t * P, (t + 1) * P)
+            for u in range(2):
+                half = slice(u * HALF, (u + 1) * HALF)
+                nc.tensor.matmul_mx(
+                    out=banks[t][:, half],
+                    lhsT=d_wd[:, cols].bitcast(FP8X4),
+                    lhsT_scale=d_sp[:, cols],
+                    rhs=x_wg[:, half].bitcast(FP8X4),
+                    rhs_scale=x_sg[:, half],
+                    start=True,
+                    stop=True,
+                )
+
+        w_wd = sb("w_wd", [P, 2 * N], U8, tag="x_w")
+        w_sd = sb("w_sd", [P, N], U8)
+        nc.vector.tensor_copy(
+            w_wd[:].rearrange("p (t m b) -> p t m b", t=PACK, b=2), w_w[:].rearrange("p (m t b) -> p t m b", t=PACK, b=2)
+        )
+        nc.vector.tensor_copy(w_sd[:].rearrange("p (t m) -> p t m", t=PACK), w_s[:].rearrange("p (m t) -> p t m", t=PACK))
+        gain16 = sb("gain16", [P, PACK], F32)
+        nc.gpsimd.tensor_scalar(gain16[:], gain[:], 0.0625, 0.0, ALU.mult, ALU.add)
+
+        ds = [sb(f"ds{t}", [P, S], F32) for t in range(PACK)]
+        neg = [sb(f"neg{t}", [P, W], F32) for t in range(PACK)]
+        old = [sb(f"old{t}", [P, W], F32) for t in range(PACK)]
+        ra = [sb(f"ra{t}", [P, W], F32) for t in range(PACK)]
+        pairs = sb("pairs", [P, 2, S, 2], BF16)
+
+        def fetch_pa(t):
+            nc.scalar.activation(neg[t][:], ds[t][:].indirect(n2_t[:]), ACT.Copy, scale=-0.5)
+
+        nc.scalar.copy(ds[0][:], banks[0][:])
+        for t in range(1, PACK):
+            nc.vector.tensor_copy(ds[t][:], banks[t][:])
+        for t in (0, 1):
+            fetch_pa(t)
+            nc.vector.tensor_tensor(old[t][:], ds[t][:].indirect(n1_t[:]), neg[t][:], ALU.add)
+        for t in (0, 1):
+            nc.vector.scalar_tensor_tensor(ra[t][:], neg[t][:], -1.0, old[t][:], ALU.mult, ALU.min)
+        for t in (2, 3):
+            fetch_pa(t)
+            nc.scalar.activation(old[t][:], ds[t][:].indirect(n1_t[:]), ACT.Copy)
+        for t in (0, 1):
+            nc.scalar.activation(ds[t][:].indirect(n1_t[:]), ra[t][:], ACT.Copy)
+        for t in (0, 1):
+            nc.scalar.activation(pairs[:, 0, :, t], ds[t][:], ACT.Copy, scale=gain16[:, t : t + 1])
+        for t in (2, 3):
+            nc.vector.scalar_tensor_tensor(ra[t][:], neg[t][:], -2.0, old[t][:], ALU.mult, ALU.min)
+        for t in (2, 3):
+            for a, b in ((0, 192), (192, W)):
+                nc.vector.tensor_tensor(
+                    ds[t][:].indirect(n1_t[:, a // 16 : b // 16]), ra[t][:, a:b], neg[t][:, a:b], ALU.add
+                )
+        for t in (2, 3):
+            nc.vector.tensor_scalar(pairs[:, 1, :, t - 2], ds[t][:], gain16[:, t : t + 1], None, ALU.mult)
+
+        z = [sb(f"z{u}", [P, HALF, PACK], BF16) for u in range(2)]
+        z_w = [sb(f"z_w{u}", [P, HALF], U32) for u in range(2)]
+        z_s = [sb(f"z_s{u}", [P, HALF], U8) for u in range(2)]
+        pair_words = pairs[:].rearrange("p u c e -> p u (c e)").bitcast(I32)
+        for u in range(2):
+            nc.vector.tensor_copy(
+                z[u][:].rearrange("p c t -> p (c t)").bitcast(I32).rearrange("p (c u) -> p c u", u=2),
+                pair_words[:, :, u * HALF : (u + 1) * HALF].rearrange("p u c -> p c u"),
+            )
+        for u in range(2):
+            nc.vector.quantize_mx(
+                out=z_w[u][:].bitcast(FP8X4), scales=z_s[u][:], in_=z[u][:].rearrange("p c t -> p (c t)")
+            )
+
+        banks2 = [psum.tile([P, S], F32, name=f"bank2_{t}") for t in range(PACK)]
+        for t in range(PACK):
+            for u in range(2):
+                half = slice(u * HALF, (u + 1) * HALF)
+                nc.tensor.matmul_mx(
+                    out=banks2[t][:, half],
+                    lhsT=w_wd[:, 2 * t * P : 2 * (t + 1) * P].bitcast(FP4X4),
+                    lhsT_scale=w_sd[:, t * P : (t + 1) * P],
+                    rhs=z_w[u][:].bitcast(FP8X4),
+                    rhs_scale=z_s[u][:],
+                    start=True,
+                    stop=True,
+                )
+
+        h2 = [sb(f"h2_{t}", [P, S], F32) for t in range(PACK)]
+        for t in range(PACK):
+            nc.vector.tensor_copy(h2[t][:], banks2[t][:])
+
+        y_s = sb("y_s", [P, S], U8)
+        gates = [sb(f"gate{i}", [P, HALF], F32) for i in range(3)]
+        out_rows = out_0.rearrange("(p t) j -> p t j", t=PACK)
+        out_words = out_1[0].rearrange("p c t -> p (c t)").bitcast(I32)
+        for u, (a, b) in enumerate(((0, 256), (256, 384), (384, S))):
+            y = sb(f"y{u}", [P, PACK, b - a], F32)
+            for t in range(PACK):
+                gate = gates[(PACK * u + t) % 3][:, 0 : b - a]
+                nc.scalar.activation(gate, h2[t][:].indirect(n3_t[:, a // 16 : b // 16]), ACT.Sigmoid)
+                nc.vector.tensor_tensor(y[:, t, :], h2[t][:, a:b], gate, ALU.mult)
+            nc.sync.dma_start(out_rows[:, :, a:b], y[:])
+            y_b = sb(f"y_b{u}", [P, b - a, PACK], BF16)
+            y_w = sb(f"y_w{u}", [P, b - a], U32)
+            nc.vector.tensor_copy(y_b[:], y[:].rearrange("p t c -> p c t"))
+            nc.vector.quantize_mx(
+                out=y_w[:].bitcast(FP8X4), scales=y_s[:, a:b], in_=y_b[:].rearrange("p c t -> p (c t)")
+            )
+            nc.sync.dma_start(out_words[:, a:b], y_w[:].bitcast(I32))
+        for r in range(4):
+            queue = nc.scalar if r % 2 == 0 else nc.sync
+            queue.dma_start(out_2[0][r:16:4, :].bitcast(I32), y_s[r:P:32, :].bitcast(I32))

@@ -41,16 +41,15 @@ def tile_picked_pqlaykmingate_none_po_kernel(
         x_w = sb("x_w", [P, T], U32)
         d_s = sb("d_s", [P, G], U8)
         x_s = sb("x_s", [P, T], U8)
-        w_w = sb("w_w", [P, 2 * N], U8)
         gain = sb("gain", [P, PACK], F32)
 
-        nc.vector.memset(d_s[:].bitcast(I32), 0)
+        w_s = sb("w_s", [P, N], U8)
         nc.vector.memset(x_s[:].bitcast(I32), 0)
+        nc.gpsimd.memset(w_s[:].bitcast(I32), 0)
 
         nc.sync.dma_start(k1_t[:], k1)
+        nc.sync.dma_start(d_s[:].bitcast(I32), d_scales[0].bitcast(I32).unsqueeze(1).to_broadcast([16, 8, G // 4]))
         nc.sync.dma_start(d_w[:].bitcast(I32), d_words[0].rearrange("p n t -> p (n t)").bitcast(I32))
-        for r in range(2):
-            nc.scalar.dma_start(d_s[r:P:16, :].bitcast(I32), d_scales[0][r:16:2, :].bitcast(I32))
         nc.sync.dma_start(offs_t[:], offs)
         nc.sync.dma_start(n2_t[:], n2)
         nc.sync.dma_start(n1_t[:], n1)
@@ -58,59 +57,55 @@ def tile_picked_pqlaykmingate_none_po_kernel(
         nc.sync.dma_start(x_w[:].bitcast(I32), x_words[0].rearrange("p n t -> p (n t)").bitcast(I32))
         for r in range(4):
             nc.scalar.dma_start(x_s[r:P:32, :].bitcast(I32), x_scales[0][r:16:4, :].bitcast(I32))
-        nc.gpsimd.dma_start(w_w[:].bitcast(I32), w1_words[0].bitcast(I32))
+        for r in range(4):
+            nc.gpsimd.dma_start(w_s[r:P:32, :].bitcast(I32), w1_scales[0][r:16:4, :].bitcast(I32))
         nc.gpsimd.dma_start(gain[:], gn.rearrange("(p t) o -> p (t o)", t=PACK))
 
         d_sg = sb("d_sg", [P, H], U8, tag="picked")
-        d_sd = sb("d_sd", [P, H], U8)
         d_sp = sb("d_sp", [P, H], U8)
         nc.vector.tensor_copy(d_sg[:], d_s[:].indirect(k1_t[:]))
-        nc.vector.tensor_copy(d_sd[:].rearrange("p (t m) -> p t m", t=PACK), d_sg[:].rearrange("p (m t) -> p t m", t=PACK))
-        nc.vector.tensor_copy(d_sp[:].bitcast(I32), d_sd[:].bitcast(I32))
-        for r in range(2):
-            nc.scalar.dma_start(d_sp[2 + r : P : 32, :].bitcast(I32), d_sd[16 + r : P : 32, :].bitcast(I32))
-
-        w_s = sb("w_s", [P, N], U8, tag="d_sd")
-        nc.gpsimd.memset(w_s[:].bitcast(I32), 0)
-        for r in range(4):
-            nc.sync.dma_start(w_s[r:P:32, :].bitcast(I32), w1_scales[0][r:16:4, :].bitcast(I32))
+        nc.vector.tensor_copy(d_sp[:].rearrange("p (t m) -> p t m", t=PACK), d_sg[:].rearrange("p (m t) -> p t m", t=PACK))
+        for r in range(1, 4):
+            nc.scalar.dma_start(d_sp[r:P:32, :].bitcast(I32), d_sp[8 * r : P : 32, :].bitcast(I32))
 
         d_wg = sb("d_wg", [P, H], U32, tag="picked")
         d_wd = sb("d_wd", [P, H], U32)
         nc.vector.tensor_copy(d_wg[:], d_w[:].indirect(k1_t[:]))
         nc.vector.tensor_copy(
-            d_wd[:].bitcast(I32).rearrange("p (t m) -> p t m", t=PACK),
-            d_wg[:].bitcast(I32).rearrange("p (m t) -> p t m", t=PACK),
+            d_wd[:].bitcast(I32).rearrange("p (t m) -> p m t", t=PACK),
+            d_wg[:].bitcast(I32).rearrange("p (m t) -> p m t", t=PACK),
         )
-        x_sg = sb("x_sg", [P, S], U8, tag="picked")
-        nc.vector.tensor_copy(x_sg[:], x_s[:].indirect(offs_t[:]))
+        w_w = sb("w_w", [P, 2 * N], U8, tag="d_w")
+        nc.sync.dma_start(w_w[:].bitcast(I32), w1_words[0].bitcast(I32))
+        x_sp = sb("x_sp", [P, S], U8, tag="picked")
+        nc.vector.tensor_copy(x_sp[:], x_s[:].indirect(offs_t[:]))
         x_wg = sb("x_wg", [P, S], U32, tag="x_s")
         for u in range(2):
             nc.vector.tensor_copy(
                 x_wg[:, u * HALF : (u + 1) * HALF], x_w[:].indirect(offs_t[:, u * HALF // 16 : (u + 1) * HALF // 16])
             )
 
-        banks = [psum.tile([P, S], F32, name=f"bank{t}") for t in range(PACK)]
+        banks = [[psum.tile([P, HALF], F32, name=f"h_bank{t}_{u}", tag=f"bank{t}_{u}") for u in range(2)] for t in range(PACK)]
         for t in range(PACK):
             cols = slice(t * P, (t + 1) * P)
             for u in range(2):
                 half = slice(u * HALF, (u + 1) * HALF)
                 nc.tensor.matmul_mx(
-                    out=banks[t][:, half],
+                    out=banks[t][u][:],
                     lhsT=d_wd[:, cols].bitcast(FP8X4),
                     lhsT_scale=d_sp[:, cols],
                     rhs=x_wg[:, half].bitcast(FP8X4),
-                    rhs_scale=x_sg[:, half],
+                    rhs_scale=x_sp[:, half],
                     start=True,
                     stop=True,
                 )
 
         w_wd = sb("w_wd", [P, 2 * N], U8, tag="x_w")
-        w_sd = sb("w_sd", [P, N], U8)
         nc.vector.tensor_copy(
             w_wd[:].rearrange("p (t m b) -> p t m b", t=PACK, b=2), w_w[:].rearrange("p (m t b) -> p t m b", t=PACK, b=2)
         )
-        nc.vector.tensor_copy(w_sd[:].rearrange("p (t m) -> p t m", t=PACK), w_s[:].rearrange("p (m t) -> p t m", t=PACK))
+        w_sp = sb("w_sp", [P, N], U8, tag="d_w")
+        nc.vector.tensor_copy(w_sp[:].rearrange("p (t m) -> p t m", t=PACK), w_s[:].rearrange("p (m t) -> p t m", t=PACK))
         gain16 = sb("gain16", [P, PACK], F32)
         nc.gpsimd.tensor_scalar(gain16[:], gain[:], 0.0625, 0.0, ALU.mult, ALU.add)
 
@@ -123,9 +118,10 @@ def tile_picked_pqlaykmingate_none_po_kernel(
         def fetch_pa(t):
             nc.scalar.activation(neg[t][:], ds[t][:].indirect(n2_t[:]), ACT.Copy, scale=-0.5)
 
-        nc.scalar.copy(ds[0][:], banks[0][:])
-        for t in range(1, PACK):
-            nc.vector.tensor_copy(ds[t][:], banks[t][:])
+        for t in range(PACK):
+            for u in range(2):
+                leave = nc.scalar.copy if t < 2 else nc.vector.tensor_copy
+                leave(ds[t][:, u * HALF : (u + 1) * HALF], banks[t][u][:])
         for t in (0, 1):
             fetch_pa(t)
             nc.vector.tensor_tensor(old[t][:], ds[t][:].indirect(n1_t[:]), neg[t][:], ALU.add)
@@ -162,14 +158,14 @@ def tile_picked_pqlaykmingate_none_po_kernel(
                 out=z_w[u][:].bitcast(FP8X4), scales=z_s[u][:], in_=z[u][:].rearrange("p c t -> p (c t)")
             )
 
-        banks2 = [psum.tile([P, S], F32, name=f"bank2_{t}") for t in range(PACK)]
+        banks2 = [psum.tile([P, S], F32, name=f"h2_bank{t}", tag=f"bank{t}_0") for t in range(PACK)]
         for t in range(PACK):
             for u in range(2):
                 half = slice(u * HALF, (u + 1) * HALF)
                 nc.tensor.matmul_mx(
                     out=banks2[t][:, half],
                     lhsT=w_wd[:, 2 * t * P : 2 * (t + 1) * P].bitcast(FP4X4),
-                    lhsT_scale=w_sd[:, t * P : (t + 1) * P],
+                    lhsT_scale=w_sp[:, t * P : (t + 1) * P],
                     rhs=z_w[u][:].bitcast(FP8X4),
                     rhs_scale=z_s[u][:],
                     start=True,
@@ -181,19 +177,22 @@ def tile_picked_pqlaykmingate_none_po_kernel(
             nc.vector.tensor_copy(h2[t][:], banks2[t][:])
 
         y_s = sb("y_s", [P, S], U8)
-        gates = [sb(f"gate{i}", [P, HALF], F32) for i in range(3)]
+        gates = sb("gates", [P, PACK * HALF], F32)
         out_rows = out_0.rearrange("(p t) j -> p t j", t=PACK)
         out_words = out_1[0].rearrange("p c t -> p (c t)").bitcast(I32)
         for u, (a, b) in enumerate(((0, 256), (256, 384), (384, S))):
             y = sb(f"y{u}", [P, PACK, b - a], F32)
             for t in range(PACK):
-                gate = gates[(PACK * u + t) % 3][:, 0 : b - a]
+                at = t * HALF if u == 0 else HALF + (P * (PACK * (u - 1) + t)) % (3 * HALF)
+                gate = gates[:, at : at + b - a]
                 nc.scalar.activation(gate, h2[t][:].indirect(n3_t[:, a // 16 : b // 16]), ACT.Sigmoid)
                 nc.vector.tensor_tensor(y[:, t, :], h2[t][:, a:b], gate, ALU.mult)
             nc.sync.dma_start(out_rows[:, :, a:b], y[:])
             y_b = sb(f"y_b{u}", [P, b - a, PACK], BF16)
             y_w = sb(f"y_w{u}", [P, b - a], U32)
-            nc.vector.tensor_copy(y_b[:], y[:].rearrange("p t c -> p c t"))
+            nc.vector.tensor_copy(
+                y_b[:].rearrange("p (c i) t -> p c t i", i=4), y[:].rearrange("p t (c i) -> p c t i", i=4)
+            )
             nc.vector.quantize_mx(
                 out=y_w[:].bitcast(FP8X4), scales=y_s[:, a:b], in_=y_b[:].rearrange("p c t -> p (c t)")
             )

@@ -43,22 +43,18 @@ def tile_picked_pqlaykmingate_none_po_kernel(
         x_s = sb("x_s", [P, T], U8)
         gain = sb("gain", [P, PACK], F32)
 
-        w_s = sb("w_s", [P, N], U8)
         nc.vector.memset(x_s[:].bitcast(I32), 0)
-        nc.gpsimd.memset(w_s[:].bitcast(I32), 0)
 
         nc.sync.dma_start(k1_t[:], k1)
         nc.sync.dma_start(d_s[:].bitcast(I32), d_scales[0].bitcast(I32).unsqueeze(1).to_broadcast([16, 8, G // 4]))
-        nc.sync.dma_start(d_w[:].bitcast(I32), d_words[0].rearrange("p n t -> p (n t)").bitcast(I32))
         nc.sync.dma_start(offs_t[:], offs)
+        nc.sync.dma_start(d_w[:].bitcast(I32), d_words[0].rearrange("p n t -> p (n t)").bitcast(I32))
+        for q in range(4):
+            nc.scalar.dma_start(x_s[32 * q : 32 * q + 4, :].bitcast(I32), x_scales[0][4 * q : 4 * q + 4, :].bitcast(I32))
         nc.sync.dma_start(n2_t[:], n2)
         nc.sync.dma_start(n1_t[:], n1)
-        nc.sync.dma_start(n3_t[:], n3)
         nc.sync.dma_start(x_w[:].bitcast(I32), x_words[0].rearrange("p n t -> p (n t)").bitcast(I32))
-        for r in range(4):
-            nc.scalar.dma_start(x_s[r:P:32, :].bitcast(I32), x_scales[0][r:16:4, :].bitcast(I32))
-        for r in range(4):
-            nc.gpsimd.dma_start(w_s[r:P:32, :].bitcast(I32), w1_scales[0][r:16:4, :].bitcast(I32))
+        nc.sync.dma_start(n3_t[:], n3)
         nc.gpsimd.dma_start(gain[:], gn.rearrange("(p t) o -> p (t o)", t=PACK))
 
         d_sg = sb("d_sg", [P, H], U8, tag="picked")
@@ -75,9 +71,13 @@ def tile_picked_pqlaykmingate_none_po_kernel(
             d_wd[:].bitcast(I32).rearrange("p (t m) -> p m t", t=PACK),
             d_wg[:].bitcast(I32).rearrange("p (m t) -> p m t", t=PACK),
         )
-        w_w = sb("w_w", [P, 2 * N], U8, tag="d_w")
+        w_s = sb("w_s", [P, N], U8, tag="d_w")
+        nc.gpsimd.memset(w_s[:].bitcast(I32), 0)
+        for q in range(4):
+            nc.sync.dma_start(w_s[32 * q : 32 * q + 4, :].bitcast(I32), w1_scales[0][4 * q : 4 * q + 4, :].bitcast(I32))
+        w_w = sb("w_w", [P, 2 * N], U8, tag="picked")
         nc.sync.dma_start(w_w[:].bitcast(I32), w1_words[0].bitcast(I32))
-        x_sp = sb("x_sp", [P, S], U8, tag="picked")
+        x_sp = sb("x_sp", [P, S], U8)
         nc.vector.tensor_copy(x_sp[:], x_s[:].indirect(offs_t[:]))
         x_wg = sb("x_wg", [P, S], U32, tag="x_s")
         for u in range(2):
@@ -104,7 +104,7 @@ def tile_picked_pqlaykmingate_none_po_kernel(
         nc.vector.tensor_copy(
             w_wd[:].rearrange("p (t m b) -> p t m b", t=PACK, b=2), w_w[:].rearrange("p (m t b) -> p t m b", t=PACK, b=2)
         )
-        w_sp = sb("w_sp", [P, N], U8, tag="d_w")
+        w_sp = sb("w_sp", [P, N], U8, tag="picked")
         nc.vector.tensor_copy(w_sp[:].rearrange("p (t m) -> p t m", t=PACK), w_s[:].rearrange("p (m t) -> p t m", t=PACK))
         gain16 = sb("gain16", [P, PACK], F32)
         nc.gpsimd.tensor_scalar(gain16[:], gain[:], 0.0625, 0.0, ALU.mult, ALU.add)
@@ -158,12 +158,11 @@ def tile_picked_pqlaykmingate_none_po_kernel(
                 out=z_w[u][:].bitcast(FP8X4), scales=z_s[u][:], in_=z[u][:].rearrange("p c t -> p (c t)")
             )
 
-        banks2 = [psum.tile([P, S], F32, name=f"h2_bank{t}", tag=f"bank{t}_0") for t in range(PACK)]
+        banks2 = [[psum.tile([P, HALF], F32, name=f"h2_bank{t}_{u}", tag=f"bank{t}_{u}") for u in range(2)] for t in range(PACK)]
         for t in range(PACK):
             for u in range(2):
-                half = slice(u * HALF, (u + 1) * HALF)
                 nc.tensor.matmul_mx(
-                    out=banks2[t][:, half],
+                    out=banks2[t][u][:],
                     lhsT=w_wd[:, 2 * t * P : 2 * (t + 1) * P].bitcast(FP4X4),
                     lhsT_scale=w_sp[:, t * P : (t + 1) * P],
                     rhs=z_w[u][:].bitcast(FP8X4),
@@ -174,7 +173,8 @@ def tile_picked_pqlaykmingate_none_po_kernel(
 
         h2 = [sb(f"h2_{t}", [P, S], F32) for t in range(PACK)]
         for t in range(PACK):
-            nc.vector.tensor_copy(h2[t][:], banks2[t][:])
+            for u in range(2):
+                nc.vector.tensor_copy(h2[t][:, u * HALF : (u + 1) * HALF], banks2[t][u][:])
 
         y_s = sb("y_s", [P, S], U8)
         gates = sb("gates", [P, PACK * HALF], F32)
@@ -197,6 +197,6 @@ def tile_picked_pqlaykmingate_none_po_kernel(
                 out=y_w[:].bitcast(FP8X4), scales=y_s[:, a:b], in_=y_b[:].rearrange("p c t -> p (c t)")
             )
             nc.sync.dma_start(out_words[:, a:b], y_w[:].bitcast(I32))
-        for r in range(4):
-            queue = nc.scalar if r % 2 == 0 else nc.sync
-            queue.dma_start(out_2[0][r:16:4, :].bitcast(I32), y_s[r:P:32, :].bitcast(I32))
+        for q in range(4):
+            queue = nc.scalar if q % 2 == 0 else nc.sync
+            queue.dma_start(out_2[0][4 * q : 4 * q + 4, :].bitcast(I32), y_s[32 * q : 32 * q + 4, :].bitcast(I32))

@@ -43,26 +43,36 @@ def tile_picked_pqlaykmingate_none_po_kernel(
         x_s = sb("x_s", [P, T], U8)
         gain = sb("gain", [P, PACK], F32)
 
-        nc.vector.memset(x_s[:].bitcast(I32), 0)
+        w_s = sb("w_s", [P, N], U8)
+        w_w = sb("w_w", [P, 2 * N], U8)
+
+        def load_scales(tile, rows):
+            width = rows.shape[1] // 4
+            nc.sync.dma_start(tile[:].bitcast(I32), rows.bitcast(I32).unsqueeze(1).to_broadcast([16, 8, width]))
 
         nc.sync.dma_start(k1_t[:], k1)
-        nc.sync.dma_start(d_s[:].bitcast(I32), d_scales[0].bitcast(I32).unsqueeze(1).to_broadcast([16, 8, G // 4]))
+        load_scales(d_s, d_scales[0])
         nc.sync.dma_start(offs_t[:], offs)
+        load_scales(x_s, x_scales[0])
         nc.sync.dma_start(d_w[:].bitcast(I32), d_words[0].rearrange("p n t -> p (n t)").bitcast(I32))
-        for q in range(4):
-            nc.scalar.dma_start(x_s[32 * q : 32 * q + 4, :].bitcast(I32), x_scales[0][4 * q : 4 * q + 4, :].bitcast(I32))
         nc.sync.dma_start(n2_t[:], n2)
         nc.sync.dma_start(n1_t[:], n1)
         nc.sync.dma_start(x_w[:].bitcast(I32), x_words[0].rearrange("p n t -> p (n t)").bitcast(I32))
         nc.sync.dma_start(n3_t[:], n3)
+        nc.sync.dma_start(w_w[:].bitcast(I32), w1_words[0].bitcast(I32))
+        load_scales(w_s, w1_scales[0])
         nc.gpsimd.dma_start(gain[:], gn.rearrange("(p t) o -> p (t o)", t=PACK))
 
-        d_sg = sb("d_sg", [P, H], U8, tag="picked")
-        d_sp = sb("d_sp", [P, H], U8)
+        d_sg = sb("d_sg", [P, H], U8)
+        x_sg = sb("x_sg", [P, S], U8, tag="picked")
+        planes = sb("planes", [P, 2 * S], U8)
+        d_sp, x_sp = planes[:, 0:S], planes[:, S : 2 * S]
         nc.vector.tensor_copy(d_sg[:], d_s[:].indirect(k1_t[:]))
-        nc.vector.tensor_copy(d_sp[:].rearrange("p (t m) -> p t m", t=PACK), d_sg[:].rearrange("p (m t) -> p t m", t=PACK))
+        nc.vector.tensor_copy(x_sg[:], x_s[:].indirect(offs_t[:]))
+        nc.vector.tensor_copy(d_sp.rearrange("p (t m) -> p t m", t=PACK), d_sg[:].rearrange("p (m t) -> p t m", t=PACK))
+        nc.vector.tensor_copy(x_sp.bitcast(I32), x_sg[:].bitcast(I32))
         for r in range(1, 4):
-            nc.scalar.dma_start(d_sp[r:P:32, :].bitcast(I32), d_sp[8 * r : P : 32, :].bitcast(I32))
+            nc.scalar.dma_start(planes[r:P:32, :].bitcast(I32), planes[8 * r : P : 32, :].bitcast(I32))
 
         d_wg = sb("d_wg", [P, H], U32, tag="picked")
         d_wd = sb("d_wd", [P, H], U32)
@@ -71,15 +81,7 @@ def tile_picked_pqlaykmingate_none_po_kernel(
             d_wd[:].bitcast(I32).rearrange("p (t m) -> p m t", t=PACK),
             d_wg[:].bitcast(I32).rearrange("p (m t) -> p m t", t=PACK),
         )
-        w_s = sb("w_s", [P, N], U8, tag="d_w")
-        nc.gpsimd.memset(w_s[:].bitcast(I32), 0)
-        for q in range(4):
-            nc.sync.dma_start(w_s[32 * q : 32 * q + 4, :].bitcast(I32), w1_scales[0][4 * q : 4 * q + 4, :].bitcast(I32))
-        w_w = sb("w_w", [P, 2 * N], U8, tag="picked")
-        nc.sync.dma_start(w_w[:].bitcast(I32), w1_words[0].bitcast(I32))
-        x_sp = sb("x_sp", [P, S], U8)
-        nc.vector.tensor_copy(x_sp[:], x_s[:].indirect(offs_t[:]))
-        x_wg = sb("x_wg", [P, S], U32, tag="x_s")
+        x_wg = sb("x_wg", [P, S], U32, tag="picked")
         for u in range(2):
             nc.vector.tensor_copy(
                 x_wg[:, u * HALF : (u + 1) * HALF], x_w[:].indirect(offs_t[:, u * HALF // 16 : (u + 1) * HALF // 16])
@@ -104,8 +106,10 @@ def tile_picked_pqlaykmingate_none_po_kernel(
         nc.vector.tensor_copy(
             w_wd[:].rearrange("p (t m b) -> p t m b", t=PACK, b=2), w_w[:].rearrange("p (m t b) -> p t m b", t=PACK, b=2)
         )
-        w_sp = sb("w_sp", [P, N], U8, tag="picked")
+        w_sp = sb("w_sp", [P, N], U8, tag="w_w")
         nc.vector.tensor_copy(w_sp[:].rearrange("p (t m) -> p t m", t=PACK), w_s[:].rearrange("p (m t) -> p t m", t=PACK))
+        for r in range(1, 4):
+            nc.sync.dma_start(w_sp[r:P:32, :].bitcast(I32), w_sp[8 * r : P : 32, :].bitcast(I32))
         gain16 = sb("gain16", [P, PACK], F32)
         nc.gpsimd.tensor_scalar(gain16[:], gain[:], 0.0625, 0.0, ALU.mult, ALU.add)
 

from contextlib import ExitStack

import concourse.mybir as mybir

K, T, S, N, G, H, W = 512, 2048, 512, 512, 2048, 512, 384
FLOPS = 2 * K * H * S + 2 * H * N * S

F32 = mybir.dt.float32
BF16 = mybir.dt.bfloat16
I32 = mybir.dt.int32
U32 = mybir.dt.uint32
U16 = mybir.dt.uint16
U8 = mybir.dt.uint8
FP8X4 = mybir.dt.float8_e4m3fn_x4
FP4X4 = mybir.dt.float4_e2m1fn_x4
ALU = mybir.AluOpType
ACT = mybir.ActivationFunctionType

P = 128
PACK = 4
HALF = S // 2


def tile_picked_pqlaykmingate_none_po_kernel(
    tc, x_words, x_scales, d_words, d_scales, gn, w1_words, w1_scales, offs, k1, n1, n2, n3, out_0, out_1, out_2
):
    nc = tc.nc
    with ExitStack() as ctx:
        keep = ctx.enter_context(tc.tile_pool(name="keep", bufs=1))
        psum = ctx.enter_context(tc.psum_pool(name="psum", bufs=1))

        def sb(name, shape, dtype, tag=None):
            return keep.tile(shape, dtype, name=name, tag=tag or name, align_bytes=64)

        k1_t = sb("k1_t", [P, H // 16], U16)
        offs_t = sb("offs_t", [P, S // 16], U16)
        n1_t = sb("n1_t", [P, W // 16], U16)
        n2_t = sb("n2_t", [P, W // 16], U16)
        n3_t = sb("n3_t", [P, S // 16], U16)
        d_w = sb("d_w", [P, G], U32)
        x_w = sb("x_w", [P, T], U32)
        d_s = sb("d_s", [P, G], U8)
        x_s = sb("x_s", [P, T], U8)
        gain = sb("gain", [P, PACK], F32)

        w_s = sb("w_s", [P, N], U8)
        w_w = sb("w_w", [P, 2 * N], U8)

        def load_scales(tile, rows):
            width = rows.shape[1] // 4
            nc.sync.dma_start(tile[:].bitcast(I32), rows.bitcast(I32).unsqueeze(1).to_broadcast([16, 8, width]))

        nc.sync.dma_start(k1_t[:], k1)
        load_scales(d_s, d_scales[0])
        nc.sync.dma_start(offs_t[:], offs)
        load_scales(x_s, x_scales[0])
        nc.sync.dma_start(d_w[:].bitcast(I32), d_words[0].rearrange("p n t -> p (n t)").bitcast(I32))
        nc.sync.dma_start(n2_t[:], n2)
        nc.sync.dma_start(n1_t[:], n1)
        nc.sync.dma_start(x_w[:].bitcast(I32), x_words[0].rearrange("p n t -> p (n t)").bitcast(I32))
        nc.sync.dma_start(n3_t[:], n3)
        nc.sync.dma_start(w_w[:].bitcast(I32), w1_words[0].bitcast(I32))
        load_scales(w_s, w1_scales[0])
        nc.gpsimd.dma_start(gain[:], gn.rearrange("(p t) o -> p (t o)", t=PACK))

        d_sg = sb("d_sg", [P, H], U8)
        x_sg = sb("x_sg", [P, S], U8, tag="picked")
        planes = sb("planes", [P, 2 * S], U8)
        d_sp, x_sp = planes[:, 0:S], planes[:, S : 2 * S]
        nc.vector.tensor_copy(d_sg[:], d_s[:].indirect(k1_t[:]))
        nc.vector.tensor_copy(x_sg[:], x_s[:].indirect(offs_t[:]))
        nc.vector.tensor_copy(d_sp.rearrange("p (t m) -> p t m", t=PACK), d_sg[:].rearrange("p (m t) -> p t m", t=PACK))
        nc.vector.tensor_copy(x_sp.bitcast(I32), x_sg[:].bitcast(I32))
        for r in range(1, 4):
            nc.scalar.dma_start(planes[r:P:32, :].bitcast(I32), planes[8 * r : P : 32, :].bitcast(I32))

        d_wg = sb("d_wg", [P, H], U32, tag="picked")
        d_wd = sb("d_wd", [P, H], U32)
        nc.vector.tensor_copy(d_wg[:], d_w[:].indirect(k1_t[:]))
        nc.vector.tensor_copy(
            d_wd[:].bitcast(I32).rearrange("p (t m) -> p m t", t=PACK),
            d_wg[:].bitcast(I32).rearrange("p (m t) -> p m t", t=PACK),
        )
        x_wg = sb("x_wg", [P, S], U32, tag="picked")
        for u in range(2):
            nc.vector.tensor_copy(
                x_wg[:, u * HALF : (u + 1) * HALF], x_w[:].indirect(offs_t[:, u * HALF // 16 : (u + 1) * HALF // 16])
            )

        banks = [[psum.tile([P, HALF], F32, name=f"h_bank{t}_{u}", tag=f"bank{t}_{u}") for u in range(2)] for t in range(PACK)]
        for t in range(PACK):
            cols = slice(t * P, (t + 1) * P)
            for u in range(2):
                half = slice(u * HALF, (u + 1) * HALF)
                nc.tensor.matmul_mx(
                    out=banks[t][u][:],
                    lhsT=d_wd[:, cols].bitcast(FP8X4),
                    lhsT_scale=d_sp[:, cols],
                    rhs=x_wg[:, half].bitcast(FP8X4),
                    rhs_scale=x_sp[:, half],
                    start=True,
                    stop=True,
                )

        w_wd = sb("w_wd", [P, 2 * N], U8, tag="x_w")
        nc.vector.tensor_copy(
            w_wd[:].rearrange("p (t m b) -> p t m b", t=PACK, b=2), w_w[:].rearrange("p (m t b) -> p t m b", t=PACK, b=2)
        )
        w_sp = sb("w_sp", [P, N], U8, tag="w_w")
        nc.vector.tensor_copy(w_sp[:].rearrange("p (t m) -> p t m", t=PACK), w_s[:].rearrange("p (m t) -> p t m", t=PACK))
        for r in range(1, 4):
            nc.sync.dma_start(w_sp[r:P:32, :].bitcast(I32), w_sp[8 * r : P : 32, :].bitcast(I32))
        gain16 = sb("gain16", [P, PACK], F32)
        nc.gpsimd.tensor_scalar(gain16[:], gain[:], 0.0625, 0.0, ALU.mult, ALU.add)

        ds = [sb(f"ds{t}", [P, S], F32) for t in range(PACK)]
        neg = [sb(f"neg{t}", [P, W], F32) for t in range(PACK)]
        old = [sb(f"old{t}", [P, W], F32) for t in range(PACK)]
        ra = [sb(f"ra{t}", [P, W], F32) for t in range(PACK)]
        pairs = sb("pairs", [P, 2, S, 2], BF16)

        def fetch_pa(t):
            nc.scalar.activation(neg[t][:], ds[t][:].indirect(n2_t[:]), ACT.Copy, scale=-0.5)

        for t in range(PACK):
            for u in range(2):
                leave = nc.scalar.copy if t < 2 else nc.vector.tensor_copy
                leave(ds[t][:, u * HALF : (u + 1) * HALF], banks[t][u][:])
        for t in (0, 1):
            fetch_pa(t)
            nc.vector.tensor_tensor(old[t][:], ds[t][:].indirect(n1_t[:]), neg[t][:], ALU.add)
        for t in (0, 1):
            nc.vector.scalar_tensor_tensor(ra[t][:], neg[t][:], -1.0, old[t][:], ALU.mult, ALU.min)
        for t in (2, 3):
            fetch_pa(t)
            nc.scalar.activation(old[t][:], ds[t][:].indirect(n1_t[:]), ACT.Copy)
        for t in (0, 1):
            nc.scalar.activation(ds[t][:].indirect(n1_t[:]), ra[t][:], ACT.Copy)
        for t in (0, 1):
            nc.scalar.activation(pairs[:, 0, :, t], ds[t][:], ACT.Copy, scale=gain16[:, t : t + 1])
        for t in (2, 3):
            nc.vector.scalar_tensor_tensor(ra[t][:], neg[t][:], -2.0, old[t][:], ALU.mult, ALU.min)
        for t in (2, 3):
            for a, b in ((0, 192), (192, W)):
                nc.vector.tensor_tensor(
                    ds[t][:].indirect(n1_t[:, a // 16 : b // 16]), ra[t][:, a:b], neg[t][:, a:b], ALU.add
                )
        for t in (2, 3):
            nc.vector.tensor_scalar(pairs[:, 1, :, t - 2], ds[t][:], gain16[:, t : t + 1], None, ALU.mult)

        z = [sb(f"z{u}", [P, HALF, PACK], BF16) for u in range(2)]
        z_w = [sb(f"z_w{u}", [P, HALF], U32) for u in range(2)]
        z_s = [sb(f"z_s{u}", [P, HALF], U8) for u in range(2)]
        pair_words = pairs[:].rearrange("p u c e -> p u (c e)").bitcast(I32)
        for u in range(2):
            nc.vector.tensor_copy(
                z[u][:].rearrange("p c t -> p (c t)").bitcast(I32).rearrange("p (c u) -> p c u", u=2),
                pair_words[:, :, u * HALF : (u + 1) * HALF].rearrange("p u c -> p c u"),
            )
        for u in range(2):
            nc.vector.quantize_mx(
                out=z_w[u][:].bitcast(FP8X4), scales=z_s[u][:], in_=z[u][:].rearrange("p c t -> p (c t)")
            )

        banks2 = [[psum.tile([P, HALF], F32, name=f"h2_bank{t}_{u}", tag=f"bank{t}_{u}") for u in range(2)] for t in range(PACK)]
        for t in range(PACK):
            for u in range(2):
                nc.tensor.matmul_mx(
                    out=banks2[t][u][:],
                    lhsT=w_wd[:, 2 * t * P : 2 * (t + 1) * P].bitcast(FP4X4),
                    lhsT_scale=w_sp[:, t * P : (t + 1) * P],
                    rhs=z_w[u][:].bitcast(FP8X4),
                    rhs_scale=z_s[u][:],
                    start=True,
                    stop=True,
                )

        h2 = [sb(f"h2_{t}", [P, S], F32) for t in range(PACK)]
        for t in range(PACK):
            for u in range(2):
                nc.vector.tensor_copy(h2[t][:, u * HALF : (u + 1) * HALF], banks2[t][u][:])

        y_s = sb("y_s", [P, S], U8)
        gates = sb("gates", [P, PACK * HALF], F32)
        out_rows = out_0.rearrange("(p t) j -> p t j", t=PACK)
        out_words = out_1[0].rearrange("p c t -> p (c t)").bitcast(I32)
        for u, (a, b) in enumerate(((0, 256), (256, 384), (384, S))):
            y = sb(f"y{u}", [P, PACK, b - a], F32)
            for t in range(PACK):
                at = t * HALF if u == 0 else HALF + (P * (PACK * (u - 1) + t)) % (3 * HALF)
                gate = gates[:, at : at + b - a]
                nc.scalar.activation(gate, h2[t][:].indirect(n3_t[:, a // 16 : b // 16]), ACT.Sigmoid)
                nc.vector.tensor_tensor(y[:, t, :], h2[t][:, a:b], gate, ALU.mult)
            nc.sync.dma_start(out_rows[:, :, a:b], y[:])
            y_b = sb(f"y_b{u}", [P, b - a, PACK], BF16)
            y_w = sb(f"y_w{u}", [P, b - a], U32)
            nc.vector.tensor_copy(
                y_b[:].rearrange("p (c i) t -> p c t i", i=4), y[:].rearrange("p t (c i) -> p c t i", i=4)
            )
            nc.vector.quantize_mx(
                out=y_w[:].bitcast(FP8X4), scales=y_s[:, a:b], in_=y_b[:].rearrange("p c t -> p (c t)")
            )
            nc.sync.dma_start(out_words[:, a:b], y_w[:].bitcast(I32))
        for q in range(4):
            queue = nc.scalar if q % 2 == 0 else nc.sync
            queue.dma_start(out_2[0][4 * q : 4 * q + 4, :].bitcast(I32), y_s[32 * q : 32 * q + 4, :].bitcast(I32))
